import numpy as np
import ml_dtypes


def mxq(x, axis, fmt="e4m3"):
    dtype, down = {"e4m3": (ml_dtypes.float8_e4m3fn, 7), "e5m2": (ml_dtypes.float8_e5m2, 14)}[fmt]
    v = np.moveaxis(np.asarray(x, np.float32).astype(ml_dtypes.bfloat16).astype(np.float64), axis, -1)
    blocks = v.reshape(v.shape[:-1] + (-1, 32))
    amax = np.abs(blocks).max(-1, keepdims=True)
    byte = np.maximum(np.where(amax > 0, np.frexp(amax)[1] - 1 + 127, 0) - down, 1)
    scale = np.exp2(byte - 127.0)
    codes = (blocks / scale).astype(np.float32).astype(dtype).astype(np.float64)
    return np.moveaxis((codes * scale).reshape(v.shape), -1, axis)


WIDE = False


def mx_kscale(k):
    if not WIDE:
        return np.ones(k)
    levels = np.array([10, -10, 5, -5, 0])
    if k % 512:
        return np.exp2(np.random.permutation(np.resize(levels, k // 32))).repeat(32)
    a = np.empty((k // 512, 16))
    for p in range(k // 512):
        a[p, :8] = np.random.permutation(np.resize(levels, 8))
        for g in range(8):
            far = levels[np.abs(levels - a[p, g]) >= 10]
            a[p, g + 8] = far[np.random.randint(len(far))]
    return np.exp2(a.ravel()).repeat(32)


def f64(x):
    return np.asarray(x).astype(np.float64)


def striped(idx):
    return np.tile(idx.reshape(-1, 16).T, (8, 1)).astype(np.uint16)


def unstriped(offs):
    return offs[:16].T.reshape(-1).astype(np.int64)


E2M1 = np.array([0.0, 0.5, 1.0, 1.5, 2.0, 3.0, 4.0, 6.0, -0.0, -0.5, -1.0, -1.5, -2.0, -3.0, -4.0, -6.0])


def pack_weight(w, fmt):
    k, n = w.shape
    w = f64(np.asarray(w, np.float32).astype(ml_dtypes.bfloat16)).reshape(k // 32, 32, n)
    amax = np.abs(w).max(1)
    if fmt == "e4m3":
        byte = np.frexp(amax)[1] - 1 + 127 - 7
    else:
        mant, ex = np.frexp(amax / 6.0)
        byte = np.where(mant > 0.5, ex, ex - 1) + 127
    byte = np.clip(np.where(amax > 0, byte, 1), 1, 254)
    scaled = (w * np.exp2(127.0 - byte)[:, None, :]).reshape(k, n).astype(np.float32)
    by_word = np.ascontiguousarray(scaled.reshape(k // 512, 128, 4, n).transpose(0, 1, 3, 2))
    if fmt == "e4m3":
        words = by_word.astype(ml_dtypes.float8_e4m3fn).view(np.uint8)
    else:
        c = by_word.astype(ml_dtypes.float4_e2m1fn).view(np.uint8) & 0xF
        words = (c[..., 0::2] | (c[..., 1::2] << 4)).reshape(k // 512, 128, 2 * n)
    return np.ascontiguousarray(words), np.ascontiguousarray(byte.astype(np.uint8).reshape(k // 512, 16, n))


def unpack_weight(words, scales, fmt):
    g, _, n = scales.shape
    words = np.ascontiguousarray(words).reshape(g, 128, n, -1)
    if fmt == "e4m3":
        vals = words.view(ml_dtypes.float8_e4m3fn).astype(np.float64)
    else:
        nib = np.empty((g, 128, n, 4), np.uint8)
        nib[..., 0::2] = words & 0xF
        nib[..., 1::2] = words >> 4
        vals = E2M1[nib]
    vals = vals * np.repeat(np.exp2(scales.astype(np.float64) - 127.0), 8, axis=1)[..., None]
    return vals.transpose(0, 1, 3, 2).reshape(g * 512, n)


K, T, E, C, N = 1536, 512, 8, 256, 128
TOP = 4


def by_expert(wq, xq):
    return np.concatenate([wq[e].T @ xq[:, e * C:(e + 1) * C] for e in range(E)], axis=1)


def setup_inputs():
    n = np.random.standard_normal
    s = mx_kscale(K)[:, None]
    deal = np.repeat(np.arange(E), C).reshape(TOP, T)[:, np.random.permutation(T)]
    deal = np.take_along_axis(deal, np.argsort(np.random.rand(TOP, T), axis=0), axis=0)
    for _ in range(8):
        s_, t_ = np.random.permutation(T).reshape(2, -1); r = np.random.randint(TOP, size=T // 2); x, y = deal[r, s_].copy(), deal[r, t_].copy()
        ok = ~((deal[:, s_] == y).any(0) | (deal[:, t_] == x).any(0)); deal[r[ok], s_[ok]] = y[ok]; deal[r[ok], t_[ok]] = x[ok]
    order = np.lexsort((np.random.rand(TOP * T), deal.reshape(-1)))
    slot_token = order % T; pos = np.empty(TOP * T, np.int64); pos[order] = np.arange(TOP * T); pos = pos.reshape(TOP, T)
    g = np.random.uniform(0.5, 1.5, (TOP, T)); g = g / g.sum(0)
    x = pack_weight(n((K, T)) * s, "e4m3")
    return {
        "x_words": x[0],
        "x_scales": x[1],
        "w": (n((E, K, N)) / np.sqrt(K) / s[None]).astype(np.float32),
        "b": (0.3 * n((N, E))).astype(np.float32),
        "gate": np.stack([np.tile(r, (N, 1)) for r in g]).astype(np.float32),
        "offs": striped(slot_token),
        "pos1": striped(pos[0]),
        "pos2": striped(pos[1]),
        "pos3": striped(pos[2]),
        "pos4": striped(pos[3]),
    }


def reference(x_words, x_scales, w, b, gate, offs, pos1, pos2, pos3, pos4):
    idx = unstriped(offs)
    xq = unpack_weight(x_words, x_scales, "e4m3")[:, idx]
    y = by_expert(mxq(f64(w), 1, "e4m3"), xq)
    y = y + np.repeat(f64(b), C, axis=1)
    return sum(f64(gate[r]) * y[:, unstriped(p)] for r, p in enumerate((pos1, pos2, pos3, pos4)))

@@ -1,0 +1,198 @@
+from contextlib import ExitStack
+
+import concourse.mybir as mybir
+
+K, T, E, C, N, TOP = 1536, 512, 8, 256, 128, 4
+SLOTS = E * C
+FLOPS = 2 * K * N * SLOTS
+
+F32 = mybir.dt.float32
+BF16 = mybir.dt.bfloat16
+I32 = mybir.dt.int32
+U32 = mybir.dt.uint32
+U16 = mybir.dt.uint16
+U8 = mybir.dt.uint8
+FP8X4 = mybir.dt.float8_e4m3fn_x4
+MULT = mybir.AluOpType.mult
+ADD = mybir.AluOpType.add
+IDENTITY = mybir.ActivationFunctionType.Identity
+
+P = 128
+PACK = 4
+K_PASS = P * PACK
+PASSES = K // K_PASS
+LIST_ROWS = 16
+HALF = E // 2
+HALF_SLOTS = HALF * C
+WIDE = 1408
+RUN = 4
+
+
+def tile_moe_pkd_lin_bias_kernel(
+    tc, x_words, x_scales, w, b, gate, offs, pos1, pos2, pos3, pos4, out
+):
+    nc = tc.nc
+    with ExitStack() as ctx:
+        keep = ctx.enter_context(tc.tile_pool(name="keep", bufs=1))
+        psum = ctx.enter_context(tc.psum_pool(name="psum", bufs=1))
+
+        offs_sb = keep.tile([P, SLOTS // LIST_ROWS], U16, name="offs_sb")
+        nc.sync.dma_start(offs_sb[:], offs)
+
+        first_col = [2 * T, 0, T]
+        words = keep.tile([P, first_col[0] + WIDE], I32, name="words", align_bytes=64)
+        scale_bytes = keep.tile([P, WIDE], U8, name="scale_bytes", align_bytes=64)
+        nc.vector.memset(scale_bytes[:].bitcast(I32), 0)
+        nc.vector.memset(words[:, PASSES * T :], 0)
+        x_rows = x_words.rearrange("o p t r -> p o (t r)").bitcast(I32)
+        nc.sync.dma_start(words[:, 2 * T : 3 * T], x_rows[:, 0, :])
+        nc.sync.dma_start(words[:, 0 : 2 * T].rearrange("p (o t) -> p o t", o=2), x_rows[:, 1:, :])
+
+        for q in range(4):
+            nc.scalar.dma_start(
+                scale_bytes[32 * q : 32 * q + 4 * PASSES, 0:T].bitcast(I32),
+                x_scales[:, 4 * q : 4 * q + 4, :].bitcast(I32),
+            )
+        raw = {}
+        for h in range(2):
+            for o in range(PASSES):
+                raw[h, o] = keep.tile([P, HALF, PACK, N], F32, name=f"raw{h}{o}")
+                nc.sync.dma_start(
+                    raw[h, o][:].rearrange("p e j n -> p e (j n)"),
+                    w[h * HALF : (h + 1) * HALF, o * K_PASS : (o + 1) * K_PASS, :].rearrange(
+                        "e (p j) n -> p e (j n)", j=PACK
+                    ),
+                )
+
+        bias = keep.tile([P, E], F32, name="bias")
+        nc.sync.dma_start(bias[:], b)
+        pos_sb = []
+        for r, pos in enumerate((pos1, pos2, pos3, pos4)):
+            pos_sb.append(keep.tile([P, T // LIST_ROWS], U16, name=f"pos{r}"))
+            nc.sync.dma_start(pos_sb[r][:], pos)
+        gate_sb = keep.tile([P, TOP, T], F32, name="gate_sb")
+        nc.sync.dma_start(gate_sb[:], gate.rearrange("r p t -> p r t"))
+
+        slot_words = [
+            keep.tile([P, SLOTS], U32, name=f"slot_words{o}", align_bytes=64) for o in range(PASSES)
+        ]
+        slot_scales = keep.tile([P, SLOTS], U8, name="slot_scales", align_bytes=64)
+        y = keep.tile([P, SLOTS], F32, name="y")
+
+        def offsets(s0, count):
+            return offs_sb[:, s0 // LIST_ROWS : (s0 + count) // LIST_ROWS]
+
+        def gather_words(o, s0, count):
+            width = T if count < T else WIDE
+            window = words[:, first_col[o] : first_col[o] + width].bitcast(U32)
+            nc.vector.tensor_copy(slot_words[o][:, s0 : s0 + count], window.indirect(offsets(s0, count)))
+
+        def gather_scales(h):
+            s0 = h * HALF_SLOTS
+            nc.vector.tensor_copy(
+                slot_scales[:, s0 : s0 + HALF_SLOTS], scale_bytes[:].indirect(offsets(s0, HALF_SLOTS))
+            )
+
+        rounded, w_codes, w_scales = {}, {}, {}
+
+        def round_weights(h, o):
+            rounded[h, o] = keep.tile([P, HALF, N, PACK], BF16, name=f"rounded{h}{o}", align_bytes=64)
+            for e in range(HALF):
+                nc.scalar.copy(
+                    rounded[h, o][:, e].rearrange("p (c i) j -> p c j i", i=RUN),
+                    raw[h, o][:, e].rearrange("p j (c i) -> p c j i", i=RUN),
+                )
+
+        def quantize_weights(h, o):
+            w_codes[h, o] = keep.tile([P, HALF * N], U32, name=f"w_codes{h}{o}", align_bytes=64)
+            w_scales[h, o] = keep.tile([P, HALF * N], U8, name=f"w_scales{h}{o}", align_bytes=64)
+            nc.vector.quantize_mx(
+                out=w_codes[h, o][:].bitcast(FP8X4),
+                scales=w_scales[h, o][:],
+                in_=rounded[h, o][:].rearrange("p e n j -> p (e n j)"),
+            )
+
+        groups = [(e * C, C, e) for e in range(E - 1)]
+        groups += [((E - 1) * C, C // 2, E - 1), ((E - 1) * C + C // 2, C // 2, 0)]
+        acc = {}
+
+        def multiply(group, o):
+            s0, count, bank = group
+            e = s0 // C
+            h, cols = e // HALF, slice((e % HALF) * N, (e % HALF + 1) * N)
+            if o == 0:
+                acc[s0] = psum.tile([P, count], F32, name=f"acc{s0}", tag=f"bank{bank}")
+            nc.tensor.matmul_mx(
+                out=acc[s0][:],
+                lhsT=w_codes[h, o][:, cols].bitcast(FP8X4),
+                lhsT_scale=w_scales[h, o][:, cols],
+                rhs=slot_words[o][:, s0 : s0 + count].bitcast(FP8X4),
+                rhs_scale=slot_scales[4 * o :, s0 : s0 + count],
+                start=(o == 0),
+                stop=(o == PASSES - 1),
+            )
+
+        def add_bias(group):
+            s0, count, bank = group
+            e = s0 // C
+            nc.scalar.activation(y[:, s0 : s0 + count], acc[s0][:], IDENTITY, bias=bias[:, e : e + 1])
+
+        first, second = groups[:HALF], groups[HALF:]
+
+        def multiply_all(part, o):
+            for group in part:
+                multiply(group, o)
+
+        round_weights(0, 0)
+        gather_words(0, 0, HALF_SLOTS)
+        gather_words(1, 0, HALF_SLOTS)
+        round_weights(0, 1)
+        gather_scales(0)
+        quantize_weights(0, 0)
+        multiply_all(first, 0)
+        gather_words(2, 0, HALF_SLOTS)
+        round_weights(0, 2)
+        quantize_weights(0, 1)
+        multiply_all(first, 1)
+        gather_words(0, HALF_SLOTS, HALF_SLOTS)
+        round_weights(1, 0)
+        quantize_weights(0, 2)
+        multiply_all(first, 2)
+        gather_words(1, HALF_SLOTS, HALF_SLOTS)
+        round_weights(1, 1)
+        quantize_weights(1, 0)
+        gather_scales(1)
+        round_weights(1, 2)
+        for group in first:
+            add_bias(group)
+        multiply_all(second, 0)
+        quantize_weights(1, 1)
+        multiply_all(second, 1)
+        gather_words(2, second[0][0], second[0][1])
+        quantize_weights(1, 2)
+        multiply(second[0], 2)
+        add_bias(second[0])
+        for group in second[1:]:
+            gather_words(2, group[0], group[1])
+            multiply(group, 2)
+            add_bias(group)
+
+        part = [keep.tile([P, T], F32, name=f"part{r}") for r in range(TOP)]
+        sum01 = keep.tile([P, T], F32, name="sum01")
+        sum012 = keep.tile([P, T], F32, name="sum012")
+        total = keep.tile([P, T], F32, name="total")
+
+        def weigh(r):
+            nc.vector.tensor_tensor(part[r][:], y[:].indirect(pos_sb[r][:]), gate_sb[:, r, :], MULT)
+
+        weigh(0)
+        weigh(1)
+        weigh(2)
+        nc.vector.tensor_tensor(sum01[:], part[0][:], part[1][:], ADD)
+        weigh(3)
+        halves = (slice(0, T // 2), slice(T // 2, T))
+        for cols in halves:
+            nc.vector.tensor_tensor(sum012[:, cols], sum01[:, cols], part[2][:, cols], ADD)
+        for cols, queue in zip(halves, (nc.sync, nc.scalar)):
+            nc.vector.tensor_tensor(total[:, cols], sum012[:, cols], part[3][:, cols], ADD)
+            queue.dma_start(out[:, cols], total[:, cols])

@@ -42,27 +42,38 @@ def tile_moe_pkd_lin_bias_kernel(
         first_col = [2 * T, 0, T]
         words = keep.tile([P, first_col[0] + WIDE], I32, name="words", align_bytes=64)
         scale_bytes = keep.tile([P, WIDE], U8, name="scale_bytes", align_bytes=64)
-        nc.vector.memset(scale_bytes[:].bitcast(I32), 0)
         nc.vector.memset(words[:, PASSES * T :], 0)
+        nc.vector.memset(scale_bytes[:].bitcast(I32), 0)
         x_rows = x_words.rearrange("o p t r -> p o (t r)").bitcast(I32)
         nc.sync.dma_start(words[:, 2 * T : 3 * T], x_rows[:, 0, :])
         nc.sync.dma_start(words[:, 0 : 2 * T].rearrange("p (o t) -> p o t", o=2), x_rows[:, 1:, :])
 
+        raw = {}
+
+        def load_weights(o, e0, count):
+            raw[o, e0] = keep.tile(
+                [P, count, PACK, N], F32, name=f"raw{o}{e0}", tag=f"stage{o}{e0}", align_bytes=64
+            )
+            nc.sync.dma_start(
+                raw[o, e0][:].rearrange("p e j n -> p e (j n)"),
+                w[e0 : e0 + count, o * K_PASS : (o + 1) * K_PASS, :].rearrange(
+                    "e (p j) n -> p e (j n)", j=PACK
+                ),
+            )
+
+        load_weights(0, 0, 2)
+        load_weights(0, 2, 2)
         for q in range(4):
-            nc.scalar.dma_start(
+            nc.sync.dma_start(
                 scale_bytes[32 * q : 32 * q + 4 * PASSES, 0:T].bitcast(I32),
                 x_scales[:, 4 * q : 4 * q + 4, :].bitcast(I32),
             )
-        raw = {}
-        for h in range(2):
-            for o in range(PASSES):
-                raw[h, o] = keep.tile([P, HALF, PACK, N], F32, name=f"raw{h}{o}")
-                nc.sync.dma_start(
-                    raw[h, o][:].rearrange("p e j n -> p e (j n)"),
-                    w[h * HALF : (h + 1) * HALF, o * K_PASS : (o + 1) * K_PASS, :].rearrange(
-                        "e (p j) n -> p e (j n)", j=PACK
-                    ),
-                )
+        load_weights(1, 0, HALF)
+        load_weights(2, 0, HALF)
+        load_weights(0, HALF, HALF)
+        load_weights(1, HALF, HALF)
+        for e in range(HALF, E):
+            load_weights(2, e, 1)
 
         bias = keep.tile([P, E], F32, name="bias")
         nc.sync.dma_start(bias[:], b)
@@ -73,44 +84,51 @@ def tile_moe_pkd_lin_bias_kernel(
         gate_sb = keep.tile([P, TOP, T], F32, name="gate_sb")
         nc.sync.dma_start(gate_sb[:], gate.rearrange("r p t -> p r t"))
 
-        slot_words = [
-            keep.tile([P, SLOTS], U32, name=f"slot_words{o}", align_bytes=64) for o in range(PASSES)
-        ]
-        slot_scales = keep.tile([P, SLOTS], U8, name="slot_scales", align_bytes=64)
         y = keep.tile([P, SLOTS], F32, name="y")
+        slot_words, slot_scales = {}, {}
 
         def offsets(s0, count):
             return offs_sb[:, s0 // LIST_ROWS : (s0 + count) // LIST_ROWS]
 
-        def gather_words(o, s0, count):
+        def gather_words(o, s0, count, tag):
             width = T if count < T else WIDE
             window = words[:, first_col[o] : first_col[o] + width].bitcast(U32)
-            nc.vector.tensor_copy(slot_words[o][:, s0 : s0 + count], window.indirect(offsets(s0, count)))
+            dense = keep.tile([P, count], U32, name=f"slot_words{o}_{s0}", tag=tag, align_bytes=64)
+            nc.vector.tensor_copy(dense[:], window.indirect(offsets(s0, count)))
+            for s in range(0, count, N):
+                slot_words[o, s0 + s] = (dense, s)
 
-        def gather_scales(h):
-            s0 = h * HALF_SLOTS
-            nc.vector.tensor_copy(
-                slot_scales[:, s0 : s0 + HALF_SLOTS], scale_bytes[:].indirect(offsets(s0, HALF_SLOTS))
-            )
+        def gather_scales(s0, tag):
+            dense = keep.tile([P, HALF_SLOTS], U8, name=f"slot_scales{s0}", tag=tag, align_bytes=64)
+            nc.vector.tensor_copy(dense[:], scale_bytes[:].indirect(offsets(s0, HALF_SLOTS)))
+            slot_scales[s0] = dense
 
-        rounded, w_codes, w_scales = {}, {}, {}
+        rounded, w_codes = {}, {}
 
-        def round_weights(h, o):
-            rounded[h, o] = keep.tile([P, HALF, N, PACK], BF16, name=f"rounded{h}{o}", align_bytes=64)
-            for e in range(HALF):
+        def round_weights(o, e0, count, into, at):
+            for e in range(count):
                 nc.scalar.copy(
-                    rounded[h, o][:, e].rearrange("p (c i) j -> p c j i", i=RUN),
-                    raw[h, o][:, e].rearrange("p j (c i) -> p c j i", i=RUN),
+                    into[:, at + e].rearrange("p (c i) j -> p c j i", i=RUN),
+                    raw[o, e0][:, e].rearrange("p j (c i) -> p c j i", i=RUN),
                 )
 
-        def quantize_weights(h, o):
-            w_codes[h, o] = keep.tile([P, HALF * N], U32, name=f"w_codes{h}{o}", align_bytes=64)
-            w_scales[h, o] = keep.tile([P, HALF * N], U8, name=f"w_scales{h}{o}", align_bytes=64)
+        def quantize_weights(o, e0, loads):
+            count = sum(loads)
+            rounded = keep.tile([P, count, N, PACK], BF16, name=f"rounded{o}{e0}", align_bytes=64)
+            at = 0
+            for size in loads:
+                round_weights(o, e0 + at, size, rounded, at)
+                at += size
+            codes = keep.tile([P, count * N], U32, name=f"w_codes{o}{e0}", align_bytes=64)
+            scales = keep.tile([P, count * N], U8, name=f"w_scales{o}{e0}", align_bytes=64)
             nc.vector.quantize_mx(
-                out=w_codes[h, o][:].bitcast(FP8X4),
-                scales=w_scales[h, o][:],
-                in_=rounded[h, o][:].rearrange("p e n j -> p (e n j)"),
+                out=codes[:].bitcast(FP8X4),
+                scales=scales[:],
+                in_=rounded[:].rearrange("p e n j -> p (e n j)"),
             )
+            for e in range(count):
+                cols = slice(e * N, (e + 1) * N)
+                w_codes[o, e0 + e] = (codes[:, cols], scales[:, cols])
 
         groups = [(e * C, C, e) for e in range(E - 1)]
         groups += [((E - 1) * C, C // 2, E - 1), ((E - 1) * C + C // 2, C // 2, 0)]
@@ -118,16 +136,17 @@ def tile_moe_pkd_lin_bias_kernel(
 
         def multiply(group, o):
             s0, count, bank = group
-            e = s0 // C
-            h, cols = e // HALF, slice((e % HALF) * N, (e % HALF + 1) * N)
+            codes, scales = w_codes[o, s0 // C]
+            dense, at = slot_words[o, s0]
+            half0 = s0 // HALF_SLOTS * HALF_SLOTS
             if o == 0:
                 acc[s0] = psum.tile([P, count], F32, name=f"acc{s0}", tag=f"bank{bank}")
             nc.tensor.matmul_mx(
                 out=acc[s0][:],
-                lhsT=w_codes[h, o][:, cols].bitcast(FP8X4),
-                lhsT_scale=w_scales[h, o][:, cols],
-                rhs=slot_words[o][:, s0 : s0 + count].bitcast(FP8X4),
-                rhs_scale=slot_scales[4 * o :, s0 : s0 + count],
+                lhsT=codes.bitcast(FP8X4),
+                lhsT_scale=scales,
+                rhs=dense[:, at : at + count].bitcast(FP8X4),
+                rhs_scale=slot_scales[half0][4 * o :, s0 - half0 : s0 - half0 + count],
                 start=(o == 0),
                 stop=(o == PASSES - 1),
             )
@@ -143,37 +162,37 @@ def tile_moe_pkd_lin_bias_kernel(
             for group in part:
                 multiply(group, o)
 
-        round_weights(0, 0)
-        gather_words(0, 0, HALF_SLOTS)
-        gather_words(1, 0, HALF_SLOTS)
-        round_weights(0, 1)
-        gather_scales(0)
-        quantize_weights(0, 0)
+        gather_words(0, 0, HALF_SLOTS, "first0")
+        gather_words(1, 0, HALF_SLOTS, "first1")
+        gather_scales(0, "first_scales")
+        quantize_weights(0, 0, (2, 2))
         multiply_all(first, 0)
-        gather_words(2, 0, HALF_SLOTS)
-        round_weights(0, 2)
-        quantize_weights(0, 1)
+        gather_words(2, 0, HALF_SLOTS, "stage02")
+        quantize_weights(1, 0, (HALF,))
         multiply_all(first, 1)
-        gather_words(0, HALF_SLOTS, HALF_SLOTS)
-        round_weights(1, 0)
-        quantize_weights(0, 2)
+        gather_words(0, HALF_SLOTS, HALF_SLOTS, "stage10")
+        quantize_weights(2, 0, (HALF,))
         multiply_all(first, 2)
-        gather_words(1, HALF_SLOTS, HALF_SLOTS)
-        round_weights(1, 1)
-        quantize_weights(1, 0)
-        gather_scales(1)
-        round_weights(1, 2)
+        gather_words(1, HALF_SLOTS, HALF_SLOTS, "stage20")
+        quantize_weights(0, HALF, (HALF,))
+        gather_scales(HALF_SLOTS, "stage04")
+        multiply_all(second[:-1], 0)
+        quantize_weights(1, HALF, (HALF,))
+        multiply_all(second[:-1], 1)
+        gather_words(2, 4 * C, C, "stage14")
+        quantize_weights(2, 4, (1,))
+        gather_words(2, 5 * C, C, "stage24")
+        quantize_weights(2, 5, (1,))
+        gather_words(2, 6 * C, C, "stage25")
+        quantize_weights(2, 6, (1,))
+        quantize_weights(2, 7, (1,))
         for group in first:
             add_bias(group)
-        multiply_all(second, 0)
-        quantize_weights(1, 1)
-        multiply_all(second, 1)
-        gather_words(2, second[0][0], second[0][1])
-        quantize_weights(1, 2)
-        multiply(second[0], 2)
-        add_bias(second[0])
-        for group in second[1:]:
-            gather_words(2, group[0], group[1])
+        multiply(second[-1], 0)
+        multiply(second[-1], 1)
+        gather_words(2, 7 * C, C // 2, "stage26")
+        gather_words(2, 7 * C + C // 2, C // 2, "stage27")
+        for group in second:
             multiply(group, 2)
             add_bias(group)
 

@@ -1,6 +1,7 @@
 from contextlib import ExitStack
 
 import concourse.mybir as mybir
+from concourse.masks import make_identity
 
 K, T, E, C, N, TOP = 1536, 512, 8, 256, 128, 4
 SLOTS = E * C
@@ -47,6 +48,9 @@ def tile_moe_pkd_lin_bias_kernel(
         x_rows = x_words.rearrange("o p t r -> p o (t r)").bitcast(I32)
         nc.sync.dma_start(words[:, 2 * T : 3 * T], x_rows[:, 0, :])
         nc.sync.dma_start(words[:, 0 : 2 * T].rearrange("p (o t) -> p o t", o=2), x_rows[:, 1:, :])
+
+        identity = keep.tile([P, P], F32, name="identity")
+        make_identity(nc, identity[:])
 
         raw = {}
 
@@ -164,10 +168,10 @@ def tile_moe_pkd_lin_bias_kernel(
 
         gather_words(0, 0, HALF_SLOTS, "first0")
         gather_words(1, 0, HALF_SLOTS, "first1")
-        gather_scales(0, "first_scales")
+        gather_words(2, 0, HALF_SLOTS, "first2")
         quantize_weights(0, 0, (2, 2))
+        gather_scales(0, "stage02")
         multiply_all(first, 0)
-        gather_words(2, 0, HALF_SLOTS, "stage02")
         quantize_weights(1, 0, (HALF,))
         multiply_all(first, 1)
         gather_words(0, HALF_SLOTS, HALF_SLOTS, "stage10")
@@ -197,21 +201,47 @@ def tile_moe_pkd_lin_bias_kernel(
             add_bias(group)
 
         part = [keep.tile([P, T], F32, name=f"part{r}") for r in range(TOP)]
-        sum01 = keep.tile([P, T], F32, name="sum01")
-        sum012 = keep.tile([P, T], F32, name="sum012")
         total = keep.tile([P, T], F32, name="total")
+        blocks = [slice(j * P, (j + 1) * P) for j in range(T // P)]
+        low, high = slice(0, T // 2), slice(T // 2, T)
 
-        def weigh(r):
-            nc.vector.tensor_tensor(part[r][:], y[:].indirect(pos_sb[r][:]), gate_sb[:, r, :], MULT)
+        def weigh(r, cols):
+            picks = pos_sb[r][:, cols.start // LIST_ROWS : cols.stop // LIST_ROWS]
+            nc.vector.tensor_tensor(part[r][:, cols], y[:].indirect(picks), gate_sb[:, r, cols], MULT)
 
-        weigh(0)
-        weigh(1)
-        weigh(2)
-        nc.vector.tensor_tensor(sum01[:], part[0][:], part[1][:], ADD)
-        weigh(3)
-        halves = (slice(0, T // 2), slice(T // 2, T))
-        for cols in halves:
-            nc.vector.tensor_tensor(sum012[:, cols], sum01[:, cols], part[2][:, cols], ADD)
-        for cols, queue in zip(halves, (nc.sync, nc.scalar)):
-            nc.vector.tensor_tensor(total[:, cols], sum012[:, cols], part[3][:, cols], ADD)
-            queue.dma_start(out[:, cols], total[:, cols])
+        turned = [psum.tile([P, P], F32, name=f"turned{j}", tag=f"bank{1 + j}") for j in range(len(blocks))]
+
+        def turn(r, j, last):
+            nc.tensor.matmul(
+                turned[j][:], part[r][:, blocks[j]], identity[:],
+                start=(r == 0), stop=last, is_transpose=True,
+            )
+
+        def turn_back(js, bank):
+            back = psum.tile([P, len(js) * P], F32, name=f"back{bank}", tag=f"bank{bank}")
+            for at, j in enumerate(js):
+                staged = keep.tile([P, P], F32, name=f"staged{j}")
+                nc.scalar.copy(staged[:], turned[j][:])
+                nc.tensor.transpose(back[:, at * P : (at + 1) * P], staged[:], identity[:])
+            return back
+
+        weigh(0, slice(0, T))
+        for j in (2, 3, 0, 1):
+            turn(0, j, False)
+        weigh(1, high)
+        for j in (2, 3):
+            turn(1, j, True)
+        back_high = turn_back((2, 3), 5)
+        for r in (1, 2):
+            weigh(r, low)
+            for j in (0, 1):
+                turn(r, j, r == 2)
+        back_low = turn_back((0, 1), 6)
+        weigh(2, high)
+        weigh(3, slice(0, T))
+        three_high = keep.tile([P, T // 2], F32, name="three_high")
+        nc.vector.tensor_tensor(three_high[:], back_high[:], part[2][:, high], ADD)
+        nc.vector.tensor_tensor(total[:, low], back_low[:], part[3][:, low], ADD)
+        nc.sync.dma_start(out[:, low], total[:, low])
+        nc.vector.tensor_tensor(total[:, high], three_high[:], part[3][:, high], ADD)
+        nc.scalar.dma_start(out[:, high], total[:, high])

from contextlib import ExitStack

import concourse.mybir as mybir
from concourse.masks import make_identity

K, T, E, C, N, TOP = 1536, 512, 8, 256, 128, 4
SLOTS = E * C
FLOPS = 2 * K * N * SLOTS

F32 = mybir.dt.float32
BF16 = mybir.dt.bfloat16
I32 = mybir.dt.int32
U32 = mybir.dt.uint32
U16 = mybir.dt.uint16
U8 = mybir.dt.uint8
FP8X4 = mybir.dt.float8_e4m3fn_x4
MULT = mybir.AluOpType.mult
ADD = mybir.AluOpType.add
IDENTITY = mybir.ActivationFunctionType.Identity

P = 128
PACK = 4
K_PASS = P * PACK
PASSES = K // K_PASS
LIST_ROWS = 16
HALF = E // 2
HALF_SLOTS = HALF * C
WIDE = 1408
RUN = 4


def tile_moe_pkd_lin_bias_kernel(
    tc, x_words, x_scales, w, b, gate, offs, pos1, pos2, pos3, pos4, out
):
    nc = tc.nc
    with ExitStack() as ctx:
        keep = ctx.enter_context(tc.tile_pool(name="keep", bufs=1))
        psum = ctx.enter_context(tc.psum_pool(name="psum", bufs=1))

        offs_sb = keep.tile([P, SLOTS // LIST_ROWS], U16, name="offs_sb")
        nc.sync.dma_start(offs_sb[:], offs)

        first_col = [2 * T, 0, T]
        words = keep.tile([P, first_col[0] + WIDE], I32, name="words", align_bytes=64)
        scale_bytes = keep.tile([P, WIDE], U8, name="scale_bytes", align_bytes=64)
        nc.vector.memset(words[:, PASSES * T :], 0)
        nc.vector.memset(scale_bytes[:].bitcast(I32), 0)
        x_rows = x_words.rearrange("o p t r -> p o (t r)").bitcast(I32)
        nc.sync.dma_start(words[:, 2 * T : 3 * T], x_rows[:, 0, :])
        nc.sync.dma_start(words[:, 0 : 2 * T].rearrange("p (o t) -> p o t", o=2), x_rows[:, 1:, :])

        identity = keep.tile([P, P], F32, name="identity")
        make_identity(nc, identity[:])

        raw = {}

        def load_weights(o, e0, count):
            raw[o, e0] = keep.tile(
                [P, count, PACK, N], F32, name=f"raw{o}{e0}", tag=f"stage{o}{e0}", align_bytes=64
            )
            nc.sync.dma_start(
                raw[o, e0][:].rearrange("p e j n -> p e (j n)"),
                w[e0 : e0 + count, o * K_PASS : (o + 1) * K_PASS, :].rearrange(
                    "e (p j) n -> p e (j n)", j=PACK
                ),
            )

        load_weights(0, 0, 2)
        load_weights(0, 2, 2)
        for q in range(4):
            nc.sync.dma_start(
                scale_bytes[32 * q : 32 * q + 4 * PASSES, 0:T].bitcast(I32),
                x_scales[:, 4 * q : 4 * q + 4, :].bitcast(I32),
            )
        load_weights(1, 0, HALF)
        load_weights(2, 0, HALF)
        load_weights(0, HALF, HALF)
        load_weights(1, HALF, HALF)
        for e in range(HALF, E):
            load_weights(2, e, 1)

        bias = keep.tile([P, E], F32, name="bias")
        nc.sync.dma_start(bias[:], b)
        pos_sb = []
        for r, pos in enumerate((pos1, pos2, pos3, pos4)):
            pos_sb.append(keep.tile([P, T // LIST_ROWS], U16, name=f"pos{r}"))
            nc.sync.dma_start(pos_sb[r][:], pos)
        gate_sb = keep.tile([P, TOP, T], F32, name="gate_sb")
        nc.sync.dma_start(gate_sb[:], gate.rearrange("r p t -> p r t"))

        y = keep.tile([P, SLOTS], F32, name="y")
        slot_words, slot_scales = {}, {}

        def offsets(s0, count):
            return offs_sb[:, s0 // LIST_ROWS : (s0 + count) // LIST_ROWS]

        def gather_words(o, s0, count, tag):
            width = T if count < T else WIDE
            window = words[:, first_col[o] : first_col[o] + width].bitcast(U32)
            dense = keep.tile([P, count], U32, name=f"slot_words{o}_{s0}", tag=tag, align_bytes=64)
            nc.vector.tensor_copy(dense[:], window.indirect(offsets(s0, count)))
            for s in range(0, count, N):
                slot_words[o, s0 + s] = (dense, s)

        def gather_scales(s0, tag):
            dense = keep.tile([P, HALF_SLOTS], U8, name=f"slot_scales{s0}", tag=tag, align_bytes=64)
            nc.vector.tensor_copy(dense[:], scale_bytes[:].indirect(offsets(s0, HALF_SLOTS)))
            slot_scales[s0] = dense

        rounded, w_codes = {}, {}

        def round_weights(o, e0, count, into, at):
            for e in range(count):
                nc.scalar.copy(
                    into[:, at + e].rearrange("p (c i) j -> p c j i", i=RUN),
                    raw[o, e0][:, e].rearrange("p j (c i) -> p c j i", i=RUN),
                )

        def quantize_weights(o, e0, loads):
            count = sum(loads)
            rounded = keep.tile([P, count, N, PACK], BF16, name=f"rounded{o}{e0}", align_bytes=64)
            at = 0
            for size in loads:
                round_weights(o, e0 + at, size, rounded, at)
                at += size
            codes = keep.tile([P, count * N], U32, name=f"w_codes{o}{e0}", align_bytes=64)
            scales = keep.tile([P, count * N], U8, name=f"w_scales{o}{e0}", align_bytes=64)
            nc.vector.quantize_mx(
                out=codes[:].bitcast(FP8X4),
                scales=scales[:],
                in_=rounded[:].rearrange("p e n j -> p (e n j)"),
            )
            for e in range(count):
                cols = slice(e * N, (e + 1) * N)
                w_codes[o, e0 + e] = (codes[:, cols], scales[:, cols])

        groups = [(e * C, C, e) for e in range(E - 1)]
        groups += [((E - 1) * C, C // 2, E - 1), ((E - 1) * C + C // 2, C // 2, 0)]
        acc = {}

        def multiply(group, o):
            s0, count, bank = group
            codes, scales = w_codes[o, s0 // C]
            dense, at = slot_words[o, s0]
            half0 = s0 // HALF_SLOTS * HALF_SLOTS
            if o == 0:
                acc[s0] = psum.tile([P, count], F32, name=f"acc{s0}", tag=f"bank{bank}")
            nc.tensor.matmul_mx(
                out=acc[s0][:],
                lhsT=codes.bitcast(FP8X4),
                lhsT_scale=scales,
                rhs=dense[:, at : at + count].bitcast(FP8X4),
                rhs_scale=slot_scales[half0][4 * o :, s0 - half0 : s0 - half0 + count],
                start=(o == 0),
                stop=(o == PASSES - 1),
            )

        def add_bias(group):
            s0, count, bank = group
            e = s0 // C
            nc.scalar.activation(y[:, s0 : s0 + count], acc[s0][:], IDENTITY, bias=bias[:, e : e + 1])

        first, second = groups[:HALF], groups[HALF:]

        def multiply_all(part, o):
            for group in part:
                multiply(group, o)

        gather_words(0, 0, HALF_SLOTS, "first0")
        gather_words(1, 0, HALF_SLOTS, "first1")
        gather_words(2, 0, HALF_SLOTS, "first2")
        quantize_weights(0, 0, (2, 2))
        gather_scales(0, "stage02")
        multiply_all(first, 0)
        quantize_weights(1, 0, (HALF,))
        multiply_all(first, 1)
        gather_words(0, HALF_SLOTS, HALF_SLOTS, "stage10")
        quantize_weights(2, 0, (HALF,))
        multiply_all(first, 2)
        gather_words(1, HALF_SLOTS, HALF_SLOTS, "stage20")
        quantize_weights(0, HALF, (HALF,))
        gather_scales(HALF_SLOTS, "stage04")
        multiply_all(second[:-1], 0)
        quantize_weights(1, HALF, (HALF,))
        multiply_all(second[:-1], 1)
        gather_words(2, 4 * C, C, "stage14")
        quantize_weights(2, 4, (1,))
        gather_words(2, 5 * C, C, "stage24")
        quantize_weights(2, 5, (1,))
        gather_words(2, 6 * C, C, "stage25")
        quantize_weights(2, 6, (1,))
        quantize_weights(2, 7, (1,))
        for group in first:
            add_bias(group)
        multiply(second[-1], 0)
        multiply(second[-1], 1)
        gather_words(2, 7 * C, C // 2, "stage26")
        gather_words(2, 7 * C + C // 2, C // 2, "stage27")
        for group in second:
            multiply(group, 2)
            add_bias(group)

        part = [keep.tile([P, T], F32, name=f"part{r}") for r in range(TOP)]
        total = keep.tile([P, T], F32, name="total")
        blocks = [slice(j * P, (j + 1) * P) for j in range(T // P)]
        low, high = slice(0, T // 2), slice(T // 2, T)

        def weigh(r, cols):
            picks = pos_sb[r][:, cols.start // LIST_ROWS : cols.stop // LIST_ROWS]
            nc.vector.tensor_tensor(part[r][:, cols], y[:].indirect(picks), gate_sb[:, r, cols], MULT)

        turned = [psum.tile([P, P], F32, name=f"turned{j}", tag=f"bank{1 + j}") for j in range(len(blocks))]

        def turn(r, j, last):
            nc.tensor.matmul(
                turned[j][:], part[r][:, blocks[j]], identity[:],
                start=(r == 0), stop=last, is_transpose=True,
            )

        def turn_back(js, bank):
            back = psum.tile([P, len(js) * P], F32, name=f"back{bank}", tag=f"bank{bank}")
            for at, j in enumerate(js):
                staged = keep.tile([P, P], F32, name=f"staged{j}")
                nc.scalar.copy(staged[:], turned[j][:])
                nc.tensor.transpose(back[:, at * P : (at + 1) * P], staged[:], identity[:])
            return back

        weigh(0, slice(0, T))
        for j in (2, 3, 0, 1):
            turn(0, j, False)
        weigh(1, high)
        for j in (2, 3):
            turn(1, j, True)
        back_high = turn_back((2, 3), 5)
        for r in (1, 2):
            weigh(r, low)
            for j in (0, 1):
                turn(r, j, r == 2)
        back_low = turn_back((0, 1), 6)
        weigh(2, high)
        weigh(3, slice(0, T))
        three_high = keep.tile([P, T // 2], F32, name="three_high")
        nc.vector.tensor_tensor(three_high[:], back_high[:], part[2][:, high], ADD)
        nc.vector.tensor_tensor(total[:, low], back_low[:], part[3][:, low], ADD)
        nc.sync.dma_start(out[:, low], total[:, low])
        nc.vector.tensor_tensor(total[:, high], three_high[:], part[3][:, high], ADD)
        nc.scalar.dma_start(out[:, high], total[:, high])
